import numpy as np, ml_dtypes
CORES = [3,1,0,2]
N = 4
T = 8
ROUTE = [[[3,2],[2,1],[3,0],[2,3],[2,3],[1,0],[1,3],[2,1]],[[2,1],[0,1],[0,2],[3,0],[0,1],[0,3],[3,0],[3,1]],[[2,1],[0,1],[0,3],[3,0],[0,1],[2,3],[2,0],[2,1]],[[2,1],[0,3],[3,0],[0,1],[3,0],[3,1],[0,1],[1,0]]]
ZW = 19
def setup_inputs(rng):
    return {"z": rng.standard_normal((N, 128, ZW), dtype=np.float32).astype(ml_dtypes.bfloat16)}
def reference(z):
    y = np.zeros((N, 128, T), np.float64)
    fill = [0] * N
    for r in range(N):
        for t in range(T):
            for e in ROUTE[r][t]:
                y[r][:, t] += z[e][:, fill[e]].astype(np.float64)
                fill[e] += 1
    return {"y": y.astype(z.dtype)}

@@ -1,0 +1,103 @@
+from concourse.mybir import AluOpType
+
+TOKENS = 8
+Z_COLS = 19
+
+SCRATCH = {
+    "zs": ("sbuf", [128, Z_COLS], "bfloat16"),
+    "land": ("sbuf", [128, 2 * TOKENS], "bfloat16"),
+    "acc": ("sbuf", [128, TOKENS], "bfloat16"),
+}
+SEMAPHORES = ["loaded", "arrived", "sent", "placed", "summed", "stored"]
+
+
+def held(route):
+    n = len(route)
+    blocks = [[[] for r in range(n)] for e in range(n)]
+    fill = [0] * n
+    for r in range(n):
+        for t, experts in enumerate(route[r]):
+            for e in experts:
+                blocks[e][r].append((t, fill[e]))
+                fill[e] += 1
+    return blocks
+
+
+def runs(pairs):
+    out = []
+    for s, t in pairs:
+        if out and out[-1][0] + out[-1][2] == s and out[-1][1] + out[-1][2] == t:
+            out[-1] = (out[-1][0], out[-1][1], out[-1][2] + 1)
+        else:
+            out.append((s, t, 1))
+    return out
+
+
+def combine_plan(route_r, where):
+    n_tok = len(route_r)
+    experts = sorted(set(e for pair in route_r for e in pair))
+    best = None
+    for choice in range(1 << n_tok):
+        passes = []
+        for flip in (0, 1):
+            moves = []
+            for e in experts:
+                pairs = [(where[(e, t)], t) for t in range(n_tok)
+                         if route_r[t][((choice >> t) & 1) ^ flip] == e]
+                moves += [(e,) + run for run in runs(pairs)]
+            passes.append(moves)
+        if best is None or len(passes[0]) + len(passes[1]) < len(best[0]) + len(best[1]):
+            best = passes
+    return best
+
+
+def rank_program(g, core, T, topo):
+    rank = T.rank_of(core)
+    if rank is None:
+        return
+    route = T.tables["ROUTE"]
+    n = len(route)
+    blocks = held(route)
+
+    def land_at(e, r):
+        return sum(len(blocks[k][r]) for k in range(e) if k != r)
+
+    g.dma_start(T.zs[:], T.z[:]).then_inc(T.sem.loaded, 16)
+    g.wait_ge(T.sem.loaded, 16)
+
+    n_sent = 0
+    for r in range(n):
+        blk = blocks[rank][r]
+        if r == rank or not blk:
+            continue
+        dst = T.cores[r]
+        rid, pid, ring = topo.addr(dst)
+        first, lo = blk[0][1], land_at(rank, r)
+        g.remote_dma(T.land[:, lo:lo + len(blk)], T.zs[:, first:first + len(blk)],
+                     remote_sem=T.sem.arrived, local_sem=T.sem.sent,
+                     pid=pid, routing_id=rid, dma_engine_mask=topo.mask(core, dst))
+        n_sent += 1
+
+    where = {}
+    for e in range(n):
+        for k, (t, zcol) in enumerate(blocks[e][rank]):
+            where[(e, t)] = zcol if e == rank else land_at(e, rank) + k
+    copies, adds = combine_plan(route[rank], where)
+
+    n_from = sum(1 for e in range(n) if e != rank and blocks[e][rank])
+    g.wait_ge(T.sem.arrived, 16 * n_from)
+
+    for e, s, t, k in copies:
+        src = T.zs if e == rank else T.land
+        g.dma_start(T.acc[:, t:t + k], src[:, s:s + k]).then_inc(T.sem.placed, 16)
+    g.wait_ge(T.sem.placed, 16 * len(copies))
+
+    for e, s, t, k in adds:
+        src = T.zs if e == rank else T.land
+        g.dma_start(T.acc[:, t:t + k], src[:, s:s + k], accum_op=AluOpType.add).then_inc(T.sem.summed, 16)
+    g.wait_ge(T.sem.summed, 16 * len(adds))
+
+    g.dma_start(T.y[:], T.acc[:]).then_inc(T.sem.stored, 16)
+    g.wait_ge(T.sem.stored, 16)
+
+    g.wait_ge(T.sem.sent, 16 * n_sent)

@@ -1,3 +1,4 @@
+from concourse.bass import DstId, RemoteDMATransfer
 from concourse.mybir import AluOpType
 
 TOKENS = 8
@@ -5,50 +6,60 @@ Z_COLS = 19
 
 SCRATCH = {
     "zs": ("sbuf", [128, Z_COLS], "bfloat16"),
-    "land": ("sbuf", [128, 2 * TOKENS], "bfloat16"),
-    "acc": ("sbuf", [128, TOKENS], "bfloat16"),
+    "lay_a": ("sbuf", [128, TOKENS], "bfloat16"),
+    "lay_b": ("sbuf", [128, TOKENS], "bfloat16"),
 }
-SEMAPHORES = ["loaded", "arrived", "sent", "placed", "summed", "stored"]
+SEMAPHORES = ["loaded", "placed", "arrived", "sent", "summed", "stored"]
 
 
-def held(route):
+def layering(route_r):
+    best = None
+    for pair in route_r:
+        nxt = []
+        for top in (0, 1):
+            now = (pair[top], pair[1 - top])
+            if best is None:
+                nxt.append((2, [now]))
+            else:
+                nxt.append(min(((cost + sum(1 for k in (0, 1) if now[k] != hist[-1][k]), hist + [now])
+                                for cost, hist in best), key=lambda c: c[0]))
+        best = nxt
+    return min(best, key=lambda c: c[0])[1]
+
+
+def all_runs(route):
     n = len(route)
-    blocks = [[[] for r in range(n)] for e in range(n)]
+    runs = [[[] for r in range(n)] for e in range(n)]
     fill = [0] * n
     for r in range(n):
-        for t, experts in enumerate(route[r]):
-            for e in experts:
-                blocks[e][r].append((t, fill[e]))
+        layers = layering(route[r])
+        for t, pair in enumerate(route[r]):
+            for e in pair:
+                layer = layers[t].index(e)
+                have = runs[e][r]
+                if have and have[-1][0] == layer and have[-1][1] + have[-1][3] == t:
+                    have[-1][3] += 1
+                else:
+                    have.append([layer, t, fill[e], 1])
                 fill[e] += 1
-    return blocks
+    return runs
 
 
-def runs(pairs):
-    out = []
-    for s, t in pairs:
-        if out and out[-1][0] + out[-1][2] == s and out[-1][1] + out[-1][2] == t:
-            out[-1] = (out[-1][0], out[-1][1], out[-1][2] + 1)
-        else:
-            out.append((s, t, 1))
-    return out
-
-
-def combine_plan(route_r, where):
-    n_tok = len(route_r)
-    experts = sorted(set(e for pair in route_r for e in pair))
-    best = None
-    for choice in range(1 << n_tok):
-        passes = []
-        for flip in (0, 1):
-            moves = []
-            for e in experts:
-                pairs = [(where[(e, t)], t) for t in range(n_tok)
-                         if route_r[t][((choice >> t) & 1) ^ flip] == e]
-                moves += [(e,) + run for run in runs(pairs)]
-            passes.append(moves)
-        if best is None or len(passes[0]) + len(passes[1]) < len(best[0]) + len(best[1]):
-            best = passes
-    return best
+def fused_calls(runs_e, e):
+    by_width = {}
+    for r, rs in enumerate(runs_e):
+        if r != e:
+            for layer, t, zcol, k in rs:
+                by_width.setdefault(k, []).append((r, layer, t, zcol, k))
+    calls = []
+    for k in sorted(by_width):
+        for i in range(0, len(by_width[k]), 16):
+            part = by_width[k][i:i + 16]
+            engines = 16
+            while engines * len(part) > 16:
+                engines //= 2
+            calls.append((engines, part))
+    return calls
 
 
 def rank_program(g, core, T, topo):
@@ -57,47 +68,39 @@ def rank_program(g, core, T, topo):
         return
     route = T.tables["ROUTE"]
     n = len(route)
-    blocks = held(route)
-
-    def land_at(e, r):
-        return sum(len(blocks[k][r]) for k in range(e) if k != r)
+    runs = all_runs(route)
+    layer_of = (T.lay_a, T.lay_b)
 
     g.dma_start(T.zs[:], T.z[:]).then_inc(T.sem.loaded, 16)
     g.wait_ge(T.sem.loaded, 16)
 
     n_sent = 0
-    for r in range(n):
-        blk = blocks[rank][r]
-        if r == rank or not blk:
-            continue
-        dst = T.cores[r]
-        rid, pid, ring = topo.addr(dst)
-        first, lo = blk[0][1], land_at(rank, r)
-        g.remote_dma(T.land[:, lo:lo + len(blk)], T.zs[:, first:first + len(blk)],
-                     remote_sem=T.sem.arrived, local_sem=T.sem.sent,
-                     pid=pid, routing_id=rid, dma_engine_mask=topo.mask(core, dst))
-        n_sent += 1
+    for engines, part in fused_calls(runs[rank], rank):
+        transfers = []
+        for i, (r, layer, t, zcol, k) in enumerate(part):
+            rid, pid, ring = topo.addr(T.cores[r])
+            transfers.append(RemoteDMATransfer(
+                dst_ids=[DstId(rid=rid, pnc=pid)],
+                dma_engine_mask=((1 << engines) - 1) << (i * engines),
+                remote_sem=T.sem.arrived,
+                src=T.zs[:, zcol:zcol + k],
+                dst=layer_of[layer][:, t:t + k]))
+            n_sent += engines
+        g.remote_dma_fused(transfers, local_sem=T.sem.sent)
 
-    where = {}
-    for e in range(n):
-        for k, (t, zcol) in enumerate(blocks[e][rank]):
-            where[(e, t)] = zcol if e == rank else land_at(e, rank) + k
-    copies, adds = combine_plan(route[rank], where)
+    for layer, t, zcol, k in runs[rank][rank]:
+        g.dma_start(layer_of[layer][:, t:t + k], T.zs[:, zcol:zcol + k]).then_inc(T.sem.placed, 16)
 
-    n_from = sum(1 for e in range(n) if e != rank and blocks[e][rank])
-    g.wait_ge(T.sem.arrived, 16 * n_from)
+    n_arrive = sum(engines
+                   for e in range(n) if e != rank
+                   for engines, part in fused_calls(runs[e], e)
+                   for move in part if move[0] == rank)
+    g.wait_ge(T.sem.placed, 16 * len(runs[rank][rank]))
+    g.wait_ge(T.sem.arrived, n_arrive)
+    g.dma_start(T.lay_a[:], T.lay_b[:], accum_op=AluOpType.add).then_inc(T.sem.summed, 16)
+    g.wait_ge(T.sem.summed, 16)
 
-    for e, s, t, k in copies:
-        src = T.zs if e == rank else T.land
-        g.dma_start(T.acc[:, t:t + k], src[:, s:s + k]).then_inc(T.sem.placed, 16)
-    g.wait_ge(T.sem.placed, 16 * len(copies))
-
-    for e, s, t, k in adds:
-        src = T.zs if e == rank else T.land
-        g.dma_start(T.acc[:, t:t + k], src[:, s:s + k], accum_op=AluOpType.add).then_inc(T.sem.summed, 16)
-    g.wait_ge(T.sem.summed, 16 * len(adds))
-
-    g.dma_start(T.y[:], T.acc[:]).then_inc(T.sem.stored, 16)
+    g.dma_start(T.y[:], T.lay_a[:]).then_inc(T.sem.stored, 16)
     g.wait_ge(T.sem.stored, 16)
 
-    g.wait_ge(T.sem.sent, 16 * n_sent)
+    g.wait_ge(T.sem.sent, n_sent)

from concourse.bass import DstId, RemoteDMATransfer
from concourse.mybir import AluOpType

TOKENS = 8
Z_COLS = 19

SCRATCH = {
    "zs": ("sbuf", [128, Z_COLS], "bfloat16"),
    "lay_a": ("sbuf", [128, TOKENS], "bfloat16"),
    "lay_b": ("sbuf", [128, TOKENS], "bfloat16"),
}
SEMAPHORES = ["loaded", "placed", "arrived", "sent", "summed", "stored"]


def layering(route_r):
    best = None
    for pair in route_r:
        nxt = []
        for top in (0, 1):
            now = (pair[top], pair[1 - top])
            if best is None:
                nxt.append((2, [now]))
            else:
                nxt.append(min(((cost + sum(1 for k in (0, 1) if now[k] != hist[-1][k]), hist + [now])
                                for cost, hist in best), key=lambda c: c[0]))
        best = nxt
    return min(best, key=lambda c: c[0])[1]


def all_runs(route):
    n = len(route)
    runs = [[[] for r in range(n)] for e in range(n)]
    fill = [0] * n
    for r in range(n):
        layers = layering(route[r])
        for t, pair in enumerate(route[r]):
            for e in pair:
                layer = layers[t].index(e)
                have = runs[e][r]
                if have and have[-1][0] == layer and have[-1][1] + have[-1][3] == t:
                    have[-1][3] += 1
                else:
                    have.append([layer, t, fill[e], 1])
                fill[e] += 1
    return runs


def fused_calls(runs_e, e):
    by_width = {}
    for r, rs in enumerate(runs_e):
        if r != e:
            for layer, t, zcol, k in rs:
                by_width.setdefault(k, []).append((r, layer, t, zcol, k))
    calls = []
    for k in sorted(by_width):
        for i in range(0, len(by_width[k]), 16):
            part = by_width[k][i:i + 16]
            engines = 16
            while engines * len(part) > 16:
                engines //= 2
            calls.append((engines, part))
    return calls


def rank_program(g, core, T, topo):
    rank = T.rank_of(core)
    if rank is None:
        return
    route = T.tables["ROUTE"]
    n = len(route)
    runs = all_runs(route)
    layer_of = (T.lay_a, T.lay_b)

    g.dma_start(T.zs[:], T.z[:]).then_inc(T.sem.loaded, 16)
    g.wait_ge(T.sem.loaded, 16)

    n_sent = 0
    for engines, part in fused_calls(runs[rank], rank):
        transfers = []
        for i, (r, layer, t, zcol, k) in enumerate(part):
            rid, pid, ring = topo.addr(T.cores[r])
            transfers.append(RemoteDMATransfer(
                dst_ids=[DstId(rid=rid, pnc=pid)],
                dma_engine_mask=((1 << engines) - 1) << (i * engines),
                remote_sem=T.sem.arrived,
                src=T.zs[:, zcol:zcol + k],
                dst=layer_of[layer][:, t:t + k]))
            n_sent += engines
        g.remote_dma_fused(transfers, local_sem=T.sem.sent)

    for layer, t, zcol, k in runs[rank][rank]:
        g.dma_start(layer_of[layer][:, t:t + k], T.zs[:, zcol:zcol + k]).then_inc(T.sem.placed, 16)

    n_arrive = sum(engines
                   for e in range(n) if e != rank
                   for engines, part in fused_calls(runs[e], e)
                   for move in part if move[0] == rank)
    g.wait_ge(T.sem.placed, 16 * len(runs[rank][rank]))
    g.wait_ge(T.sem.arrived, n_arrive)
    g.dma_start(T.lay_a[:], T.lay_b[:], accum_op=AluOpType.add).then_inc(T.sem.summed, 16)
    g.wait_ge(T.sem.summed, 16)

    g.dma_start(T.y[:], T.lay_a[:]).then_inc(T.sem.stored, 16)
    g.wait_ge(T.sem.stored, 16)

    g.wait_ge(T.sem.sent, n_sent)
